import numpy as np
import ml_dtypes


def mxq(x, axis, fmt="e4m3"):
    dtype, down = {"e4m3": (ml_dtypes.float8_e4m3fn, 7), "e5m2": (ml_dtypes.float8_e5m2, 14)}[fmt]
    v = np.moveaxis(np.asarray(x, np.float32).astype(ml_dtypes.bfloat16).astype(np.float64), axis, -1)
    blocks = v.reshape(v.shape[:-1] + (-1, 32))
    amax = np.abs(blocks).max(-1, keepdims=True)
    byte = np.maximum(np.where(amax > 0, np.frexp(amax)[1] - 1 + 127, 0) - down, 1)
    scale = np.exp2(byte - 127.0)
    codes = (blocks / scale).astype(np.float32).astype(dtype).astype(np.float64)
    return np.moveaxis((codes * scale).reshape(v.shape), -1, axis)


WIDE = False


def mx_kscale(k):
    if not WIDE:
        return np.ones(k)
    levels = np.array([10, -10, 5, -5, 0])
    if k % 512:
        return np.exp2(np.random.permutation(np.resize(levels, k // 32))).repeat(32)
    a = np.empty((k // 512, 16))
    for p in range(k // 512):
        a[p, :8] = np.random.permutation(np.resize(levels, 8))
        for g in range(8):
            far = levels[np.abs(levels - a[p, g]) >= 10]
            a[p, g + 8] = far[np.random.randint(len(far))]
    return np.exp2(a.ravel()).repeat(32)


def f64(x):
    return np.asarray(x).astype(np.float64)


def striped(idx):
    return np.tile(idx.reshape(-1, 16).T, (8, 1)).astype(np.uint16)


def unstriped(offs):
    return offs[:16].T.reshape(-1).astype(np.int64)


def pack_weight(w):
    k, n = w.shape
    w = f64(np.asarray(w, np.float32).astype(ml_dtypes.bfloat16)).reshape(k // 32, 32, n)
    amax = np.abs(w).max(1)
    byte = np.clip(np.where(amax > 0, np.frexp(amax)[1] - 1 + 127 - 7, 1), 1, 254)
    scaled = (w * np.exp2(127.0 - byte)[:, None, :]).reshape(k, n).astype(np.float32)
    words = np.ascontiguousarray(scaled.reshape(k // 512, 128, 4, n).transpose(0, 1, 3, 2)).astype(ml_dtypes.float8_e4m3fn).view(np.uint8)
    return words, np.ascontiguousarray(byte.astype(np.uint8).reshape(k // 512, 16, n))


def unpack_weight(words, scales):
    g, p, n, _ = words.shape
    vals = np.ascontiguousarray(words).view(ml_dtypes.float8_e4m3fn).astype(np.float64) * np.repeat(np.exp2(scales.astype(np.float64) - 127.0), 8, axis=1)[..., None]
    return vals.transpose(0, 1, 3, 2).reshape(g * 512, n)


def sigmoid(v):
    return 1.0 / (1.0 + np.exp(-np.maximum(v, -700.0)))


K, T, D, S, V, N = 512, 4096, 2, 1536, 768, 256


def setup_inputs():
    n = np.random.standard_normal
    s = mx_kscale(K)[:, None]
    packed = pack_weight(n((K, T)) * s)
    return {
        "x_words": packed[0],
        "x_scales": packed[1],
        "w": (n((D, K, N)) / np.sqrt(K) / s[None]).astype(np.float32),
        "b": (0.3 * n((N, 1))).astype(np.float32),
        "offs": striped(np.random.permutation(T)[:S]),
    }


def reference(x_words, x_scales, w, b, offs):
    idx = unstriped(offs)
    xq = unpack_weight(x_words, x_scales)[:, idx]
    wq = mxq(f64(w), 1, "e4m3")
    y0 = wq[0].T @ xq[:, :V]
    y1 = wq[1].T @ xq[:, V:]
    return y0 * sigmoid(y1 + f64(b))

@@ -1,0 +1,122 @@
+from contextlib import ExitStack
+
+import concourse.mybir as mybir
+
+K, T, S, V, N = 512, 4096, 1536, 768, 256
+FLOPS = 2 * K * N * S
+
+F32 = mybir.dt.float32
+BF16 = mybir.dt.bfloat16
+I32 = mybir.dt.int32
+U32 = mybir.dt.uint32
+U16 = mybir.dt.uint16
+U8 = mybir.dt.uint8
+FP8X4 = mybir.dt.float8_e4m3fn_x4
+SIGMOID = mybir.ActivationFunctionType.Sigmoid
+MULT = mybir.AluOpType.mult
+
+P = 128
+PACK = 4
+BANK = 512
+LATE = 512
+
+
+def tile_picked_pair_lin_gate_sub_p_kernel(tc, x_words, x_scales, w, b, offs, out):
+    nc = tc.nc
+    with ExitStack() as ctx:
+        keep = ctx.enter_context(tc.tile_pool(name="keep", bufs=1))
+        psum = ctx.enter_context(tc.psum_pool(name="psum", bufs=1))
+
+        offsets = keep.tile([P, S // 16], U16, name="offsets")
+        nc.sync.dma_start(offsets[:], offs)
+
+        table_scales = keep.tile([P, T], U8, name="table_scales", tag="scales_then_words", align_bytes=64)
+        nc.sync.dma_start(table_scales[112:128, :].bitcast(I32), x_scales[0].bitcast(I32))
+        nc.vector.memset(table_scales[0:112, :].bitcast(I32), 0)
+
+        table_words = keep.tile([P, T], I32, name="table_words", align_bytes=64)
+        nc.sync.dma_start(table_words[:], x_words[0].rearrange("p c r -> p (c r)").bitcast(I32))
+
+        w_raw = {}
+        for d in (1, 0):
+            w_raw[d] = keep.tile([P, PACK, N], F32, name="w_raw%d" % d)
+            nc.sync.dma_start(w_raw[d][:], w[d].rearrange("(p j) m -> p j m", j=PACK))
+
+        bias = keep.tile([P, N // P], F32, name="bias")
+        with nc.allow_non_contiguous_dma(reason="one bias value a partition"):
+            nc.scalar.dma_start(bias[:], b.rearrange("(t p) o -> p (t o)", p=P))
+
+        gathered_scales = keep.tile([P, S], U8, name="gathered_scales", align_bytes=64)
+        nc.vector.tensor_copy(gathered_scales[:], table_scales[:].indirect(offsets[:]))
+        picked_scales = keep.tile([P, S], U8, name="picked_scales", align_bytes=64)
+        nc.vector.memset(picked_scales[:].bitcast(I32), 0)
+        for q in range(4):
+            nc.sync.dma_start(
+                picked_scales[32 * q : 32 * q + 4, :].bitcast(I32),
+                gathered_scales[112 + 4 * q : 116 + 4 * q, :].bitcast(I32),
+            )
+
+        early_words = keep.tile([P, S - LATE], U32, name="early_words", tag="scales_then_words", align_bytes=64)
+        nc.vector.tensor_copy(early_words[:], table_words[:].bitcast(U32).indirect(offsets[:, LATE // 16 :]))
+
+        def round_weights(d, tag):
+            grouped = keep.tile([P, N, PACK], BF16, name="w_grouped%d" % d, tag=tag, align_bytes=64)
+            nc.scalar.copy(
+                grouped[:].rearrange("p (c i) t -> p c t i", i=4),
+                w_raw[d][:].rearrange("p t (c i) -> p c t i", i=4),
+            )
+            return grouped
+
+        def quantize(d, grouped, pieces):
+            codes = keep.tile([P, N], U32, name="w_codes%d" % d, align_bytes=64)
+            scales = keep.tile([P, N], U8, name="w_scales%d" % d, align_bytes=64)
+            flat = grouped[:].rearrange("p m t -> p (m t)")
+            width = N // pieces
+            for h in range(pieces):
+                cols = slice(h * width, (h + 1) * width)
+                nc.vector.quantize_mx(
+                    out=codes[:, cols].bitcast(FP8X4),
+                    scales=scales[:, cols],
+                    in_=flat[:, PACK * h * width : PACK * (h + 1) * width],
+                )
+            return codes, scales
+
+        grouped1 = round_weights(1, "shared")
+        grouped0 = round_weights(0, "w_grouped0")
+        codes1, scales1 = quantize(1, grouped1, 1)
+
+        late_words = keep.tile([P, LATE], U32, name="late_words", tag="shared", align_bytes=64)
+        nc.vector.tensor_copy(late_words[:], table_words[:].bitcast(U32).indirect(offsets[:, : LATE // 16]))
+        codes0, scales0 = quantize(0, grouped0, 2)
+
+        def words_of(first, count):
+            if first < LATE:
+                return late_words[:, first : first + count]
+            return early_words[:, first - LATE : first - LATE + count]
+
+        def product(name, codes, scales, m, first, count):
+            acc = psum.tile([P, count], F32, name=name)
+            cols = slice(m * P, (m + 1) * P)
+            nc.tensor.matmul_mx(
+                out=acc[:],
+                lhsT=codes[:, cols].bitcast(FP8X4),
+                lhsT_scale=scales[:, cols],
+                rhs=words_of(first, count).bitcast(FP8X4),
+                rhs_scale=picked_scales[:, first : first + count],
+                start=True,
+                stop=True,
+            )
+            return acc
+
+        pieces = [(0, BANK, V - BANK), (0, 0, BANK), (1, 0, BANK), (1, BANK, V - BANK)]
+        gates = []
+        for i, (m, v0, count) in enumerate(pieces):
+            y1 = product("y1_%d" % i, codes1, scales1, m, V + v0, count)
+            gate = keep.tile([P, count], F32, name="gate%d" % i)
+            nc.scalar.activation(gate[:], y1[:], SIGMOID, bias=bias[:, m : m + 1])
+            gates.append(gate)
+        for i, (m, v0, count) in enumerate(pieces):
+            y0 = product("y0_%d" % i, codes0, scales0, m, v0, count)
+            result = keep.tile([P, count], F32, name="result%d" % i)
+            nc.vector.tensor_tensor(result[:], y0[:], gates[i][:], MULT)
+            nc.sync.dma_start(out[m * P : (m + 1) * P, v0 : v0 + count], result[:])

@@ -31,7 +31,7 @@ def tile_picked_pair_lin_gate_sub_p_kernel(tc, x_words, x_scales, w, b, offs, ou
         nc.sync.dma_start(offsets[:], offs)
 
         table_scales = keep.tile([P, T], U8, name="table_scales", tag="scales_then_words", align_bytes=64)
-        nc.sync.dma_start(table_scales[112:128, :].bitcast(I32), x_scales[0].bitcast(I32))
+        nc.scalar.dma_start(table_scales[112:128, :].bitcast(I32), x_scales[0].bitcast(I32))
         nc.vector.memset(table_scales[0:112, :].bitcast(I32), 0)
 
         table_words = keep.tile([P, T], I32, name="table_words", align_bytes=64)
@@ -44,14 +44,18 @@ def tile_picked_pair_lin_gate_sub_p_kernel(tc, x_words, x_scales, w, b, offs, ou
 
         bias = keep.tile([P, N // P], F32, name="bias")
         with nc.allow_non_contiguous_dma(reason="one bias value a partition"):
-            nc.scalar.dma_start(bias[:], b.rearrange("(t p) o -> p (t o)", p=P))
+            nc.sync.dma_start(bias[:], b.rearrange("(t p) o -> p (t o)", p=P))
+        warm_in = keep.tile([P, 1], F32, name="warm_in")
+        warm_out = keep.tile([P, 1], F32, name="warm_out")
+        nc.gpsimd.memset(warm_in[:], 0.0)
+        nc.scalar.activation(warm_out[:], warm_in[:], SIGMOID)
 
         gathered_scales = keep.tile([P, S], U8, name="gathered_scales", align_bytes=64)
         nc.vector.tensor_copy(gathered_scales[:], table_scales[:].indirect(offsets[:]))
         picked_scales = keep.tile([P, S], U8, name="picked_scales", align_bytes=64)
         nc.vector.memset(picked_scales[:].bitcast(I32), 0)
         for q in range(4):
-            nc.sync.dma_start(
+            nc.scalar.dma_start(
                 picked_scales[32 * q : 32 * q + 4, :].bitcast(I32),
                 gathered_scales[112 + 4 * q : 116 + 4 * q, :].bitcast(I32),
             )

@@ -18,6 +18,7 @@ MULT = mybir.AluOpType.mult
 P = 128
 PACK = 4
 BANK = 512
+HALF = 256
 LATE = 512
 
 
@@ -31,8 +32,8 @@ def tile_picked_pair_lin_gate_sub_p_kernel(tc, x_words, x_scales, w, b, offs, ou
         nc.sync.dma_start(offsets[:], offs)
 
         table_scales = keep.tile([P, T], U8, name="table_scales", tag="scales_then_words", align_bytes=64)
-        nc.scalar.dma_start(table_scales[112:128, :].bitcast(I32), x_scales[0].bitcast(I32))
-        nc.vector.memset(table_scales[0:112, :].bitcast(I32), 0)
+        nc.vector.memset(table_scales[:].bitcast(I32), 0)
+        nc.scalar.dma_start(table_scales[32:96:4, :].bitcast(I32), x_scales[0].bitcast(I32))
 
         table_words = keep.tile([P, T], I32, name="table_words", align_bytes=64)
         nc.sync.dma_start(table_words[:], x_words[0].rearrange("p c r -> p (c r)").bitcast(I32))
@@ -47,7 +48,7 @@ def tile_picked_pair_lin_gate_sub_p_kernel(tc, x_words, x_scales, w, b, offs, ou
             nc.sync.dma_start(bias[:], b.rearrange("(t p) o -> p (t o)", p=P))
         warm_in = keep.tile([P, 1], F32, name="warm_in")
         warm_out = keep.tile([P, 1], F32, name="warm_out")
-        nc.gpsimd.memset(warm_in[:], 0.0)
+        nc.vector.memset(warm_in[:], 0.0)
         nc.scalar.activation(warm_out[:], warm_in[:], SIGMOID)
 
         gathered_scales = keep.tile([P, S], U8, name="gathered_scales", align_bytes=64)
@@ -57,7 +58,7 @@ def tile_picked_pair_lin_gate_sub_p_kernel(tc, x_words, x_scales, w, b, offs, ou
         for q in range(4):
             nc.scalar.dma_start(
                 picked_scales[32 * q : 32 * q + 4, :].bitcast(I32),
-                gathered_scales[112 + 4 * q : 116 + 4 * q, :].bitcast(I32),
+                gathered_scales[32 + 16 * q : 48 + 16 * q : 4, :].bitcast(I32),
             )
 
         early_words = keep.tile([P, S - LATE], U32, name="early_words", tag="scales_then_words", align_bytes=64)
@@ -98,11 +99,10 @@ def tile_picked_pair_lin_gate_sub_p_kernel(tc, x_words, x_scales, w, b, offs, ou
                 return late_words[:, first : first + count]
             return early_words[:, first - LATE : first - LATE + count]
 
-        def product(name, codes, scales, m, first, count):
-            acc = psum.tile([P, count], F32, name=name)
+        def product(acc, codes, scales, m, first, count):
             cols = slice(m * P, (m + 1) * P)
             nc.tensor.matmul_mx(
-                out=acc[:],
+                out=acc,
                 lhsT=codes[:, cols].bitcast(FP8X4),
                 lhsT_scale=scales[:, cols],
                 rhs=words_of(first, count).bitcast(FP8X4),
@@ -110,17 +110,28 @@ def tile_picked_pair_lin_gate_sub_p_kernel(tc, x_words, x_scales, w, b, offs, ou
                 start=True,
                 stop=True,
             )
-            return acc
 
-        pieces = [(0, BANK, V - BANK), (0, 0, BANK), (1, 0, BANK), (1, BANK, V - BANK)]
-        gates = []
-        for i, (m, v0, count) in enumerate(pieces):
-            y1 = product("y1_%d" % i, codes1, scales1, m, V + v0, count)
-            gate = keep.tile([P, count], F32, name="gate%d" % i)
-            nc.scalar.activation(gate[:], y1[:], SIGMOID, bias=bias[:, m : m + 1])
-            gates.append(gate)
-        for i, (m, v0, count) in enumerate(pieces):
-            y0 = product("y0_%d" % i, codes0, scales0, m, v0, count)
-            result = keep.tile([P, count], F32, name="result%d" % i)
-            nc.vector.tensor_tensor(result[:], y0[:], gates[i][:], MULT)
-            nc.sync.dma_start(out[m * P : (m + 1) * P, v0 : v0 + count], result[:])
+        wide0 = psum.tile([P, BANK], F32, name="wide0", tag="reused")
+        narrow = psum.tile([P, BANK], F32, name="narrow")
+        wide1 = psum.tile([P, BANK], F32, name="wide1")
+        gate_pieces = [
+            (0, 0, BANK, wide0[:]),
+            (0, BANK, HALF, narrow[:, :HALF]),
+            (1, BANK, HALF, narrow[:, HALF:]),
+            (1, 0, BANK, wide1[:]),
+        ]
+        for m, v0, count, y1 in gate_pieces:
+            product(y1, codes1, scales1, m, V + v0, count)
+        gates = {}
+        for m, v0, count, y1 in gate_pieces:
+            gate = keep.tile([P, count], F32, name="gate%d_%d" % (m, v0))
+            nc.scalar.activation(gate[:], y1, SIGMOID, bias=bias[:, m : m + 1])
+            for c in range(0, count, HALF):
+                gates[m, v0 + c] = gate[:, c : c + HALF]
+        for i, (m, v0) in enumerate(gates):
+            tag = "reused" if i == len(gates) - 1 else "y0_%d" % i
+            y0 = psum.tile([P, BANK], F32, name="y0_%d" % i, tag=tag)
+            product(y0[:, :HALF], codes0, scales0, m, v0, HALF)
+            result = keep.tile([P, HALF], F32, name="result%d" % i)
+            nc.vector.tensor_tensor(result[:], y0[:, :HALF], gates[m, v0], MULT)
+            nc.sync.dma_start(out[m * P : (m + 1) * P, v0 : v0 + HALF], result[:])

@@ -32,8 +32,8 @@ def tile_picked_pair_lin_gate_sub_p_kernel(tc, x_words, x_scales, w, b, offs, ou
         nc.sync.dma_start(offsets[:], offs)
 
         table_scales = keep.tile([P, T], U8, name="table_scales", tag="scales_then_words", align_bytes=64)
-        nc.vector.memset(table_scales[:].bitcast(I32), 0)
-        nc.scalar.dma_start(table_scales[32:96:4, :].bitcast(I32), x_scales[0].bitcast(I32))
+        nc.scalar.dma_start(table_scales[112:128, :].bitcast(I32), x_scales[0].bitcast(I32))
+        nc.vector.memset(table_scales[0:112, :].bitcast(I32), 0)
 
         table_words = keep.tile([P, T], I32, name="table_words", align_bytes=64)
         nc.sync.dma_start(table_words[:], x_words[0].rearrange("p c r -> p (c r)").bitcast(I32))
@@ -48,7 +48,7 @@ def tile_picked_pair_lin_gate_sub_p_kernel(tc, x_words, x_scales, w, b, offs, ou
             nc.sync.dma_start(bias[:], b.rearrange("(t p) o -> p (t o)", p=P))
         warm_in = keep.tile([P, 1], F32, name="warm_in")
         warm_out = keep.tile([P, 1], F32, name="warm_out")
-        nc.vector.memset(warm_in[:], 0.0)
+        nc.gpsimd.memset(warm_in[:], 0.0)
         nc.scalar.activation(warm_out[:], warm_in[:], SIGMOID)
 
         gathered_scales = keep.tile([P, S], U8, name="gathered_scales", align_bytes=64)
@@ -58,41 +58,38 @@ def tile_picked_pair_lin_gate_sub_p_kernel(tc, x_words, x_scales, w, b, offs, ou
         for q in range(4):
             nc.scalar.dma_start(
                 picked_scales[32 * q : 32 * q + 4, :].bitcast(I32),
-                gathered_scales[32 + 16 * q : 48 + 16 * q : 4, :].bitcast(I32),
+                gathered_scales[112 + 4 * q : 116 + 4 * q, :].bitcast(I32),
             )
 
         early_words = keep.tile([P, S - LATE], U32, name="early_words", tag="scales_then_words", align_bytes=64)
         nc.vector.tensor_copy(early_words[:], table_words[:].bitcast(U32).indirect(offsets[:, LATE // 16 :]))
 
-        def round_weights(d, tag):
-            grouped = keep.tile([P, N, PACK], BF16, name="w_grouped%d" % d, tag=tag, align_bytes=64)
+        def round_weights(d, m, tag):
+            grouped = keep.tile([P, P, PACK], BF16, name="grouped%d_%d" % (d, m), tag=tag, align_bytes=64)
             nc.scalar.copy(
                 grouped[:].rearrange("p (c i) t -> p c t i", i=4),
-                w_raw[d][:].rearrange("p t (c i) -> p c t i", i=4),
+                w_raw[d][:, :, m * P : (m + 1) * P].rearrange("p t (c i) -> p c t i", i=4),
             )
             return grouped
 
-        def quantize(d, grouped, pieces):
-            codes = keep.tile([P, N], U32, name="w_codes%d" % d, align_bytes=64)
-            scales = keep.tile([P, N], U8, name="w_scales%d" % d, align_bytes=64)
-            flat = grouped[:].rearrange("p m t -> p (m t)")
-            width = N // pieces
-            for h in range(pieces):
-                cols = slice(h * width, (h + 1) * width)
-                nc.vector.quantize_mx(
-                    out=codes[:, cols].bitcast(FP8X4),
-                    scales=scales[:, cols],
-                    in_=flat[:, PACK * h * width : PACK * (h + 1) * width],
-                )
-            return codes, scales
+        def quantize(grouped, codes, scales):
+            nc.vector.quantize_mx(out=codes.bitcast(FP8X4), scales=scales, in_=grouped[:].rearrange("p m t -> p (m t)"))
 
-        grouped1 = round_weights(1, "shared")
-        grouped0 = round_weights(0, "w_grouped0")
-        codes1, scales1 = quantize(1, grouped1, 1)
+        codes1 = keep.tile([P, N], U32, name="codes1", align_bytes=64)
+        scales1 = keep.tile([P, N], U8, name="scales1", align_bytes=64)
+        codes0 = keep.tile([P, N], U32, name="codes0", align_bytes=64)
+        scales0 = keep.tile([P, N], U8, name="scales0", align_bytes=64)
+        grouped1a = round_weights(1, 0, "grouped1a")
+        grouped1b = round_weights(1, 1, "shared")
+        grouped0a = round_weights(0, 0, "grouped0a")
+        grouped0b = round_weights(0, 1, "grouped0b")
+        quantize(grouped1a, codes1[:, :P], scales1[:, :P])
+        quantize(grouped1b, codes1[:, P:], scales1[:, P:])
 
         late_words = keep.tile([P, LATE], U32, name="late_words", tag="shared", align_bytes=64)
         nc.vector.tensor_copy(late_words[:], table_words[:].bitcast(U32).indirect(offsets[:, : LATE // 16]))
-        codes0, scales0 = quantize(0, grouped0, 2)
+        quantize(grouped0a, codes0[:, :P], scales0[:, :P])
+        quantize(grouped0b, codes0[:, P:], scales0[:, P:])
 
         def words_of(first, count):
             if first < LATE:

from contextlib import ExitStack

import concourse.mybir as mybir

K, T, S, V, N = 512, 4096, 1536, 768, 256
FLOPS = 2 * K * N * S

F32 = mybir.dt.float32
BF16 = mybir.dt.bfloat16
I32 = mybir.dt.int32
U32 = mybir.dt.uint32
U16 = mybir.dt.uint16
U8 = mybir.dt.uint8
FP8X4 = mybir.dt.float8_e4m3fn_x4
SIGMOID = mybir.ActivationFunctionType.Sigmoid
MULT = mybir.AluOpType.mult

P = 128
PACK = 4
BANK = 512
HALF = 256
LATE = 512


def tile_picked_pair_lin_gate_sub_p_kernel(tc, x_words, x_scales, w, b, offs, out):
    nc = tc.nc
    with ExitStack() as ctx:
        keep = ctx.enter_context(tc.tile_pool(name="keep", bufs=1))
        psum = ctx.enter_context(tc.psum_pool(name="psum", bufs=1))

        offsets = keep.tile([P, S // 16], U16, name="offsets")
        nc.sync.dma_start(offsets[:], offs)

        table_scales = keep.tile([P, T], U8, name="table_scales", tag="scales_then_words", align_bytes=64)
        nc.scalar.dma_start(table_scales[112:128, :].bitcast(I32), x_scales[0].bitcast(I32))
        nc.vector.memset(table_scales[0:112, :].bitcast(I32), 0)

        table_words = keep.tile([P, T], I32, name="table_words", align_bytes=64)
        nc.sync.dma_start(table_words[:], x_words[0].rearrange("p c r -> p (c r)").bitcast(I32))

        w_raw = {}
        for d in (1, 0):
            w_raw[d] = keep.tile([P, PACK, N], F32, name="w_raw%d" % d)
            nc.sync.dma_start(w_raw[d][:], w[d].rearrange("(p j) m -> p j m", j=PACK))

        bias = keep.tile([P, N // P], F32, name="bias")
        with nc.allow_non_contiguous_dma(reason="one bias value a partition"):
            nc.sync.dma_start(bias[:], b.rearrange("(t p) o -> p (t o)", p=P))
        warm_in = keep.tile([P, 1], F32, name="warm_in")
        warm_out = keep.tile([P, 1], F32, name="warm_out")
        nc.gpsimd.memset(warm_in[:], 0.0)
        nc.scalar.activation(warm_out[:], warm_in[:], SIGMOID)

        gathered_scales = keep.tile([P, S], U8, name="gathered_scales", align_bytes=64)
        nc.vector.tensor_copy(gathered_scales[:], table_scales[:].indirect(offsets[:]))
        picked_scales = keep.tile([P, S], U8, name="picked_scales", align_bytes=64)
        nc.vector.memset(picked_scales[:].bitcast(I32), 0)
        for q in range(4):
            nc.scalar.dma_start(
                picked_scales[32 * q : 32 * q + 4, :].bitcast(I32),
                gathered_scales[112 + 4 * q : 116 + 4 * q, :].bitcast(I32),
            )

        early_words = keep.tile([P, S - LATE], U32, name="early_words", tag="scales_then_words", align_bytes=64)
        nc.vector.tensor_copy(early_words[:], table_words[:].bitcast(U32).indirect(offsets[:, LATE // 16 :]))

        def round_weights(d, m, tag):
            grouped = keep.tile([P, P, PACK], BF16, name="grouped%d_%d" % (d, m), tag=tag, align_bytes=64)
            nc.scalar.copy(
                grouped[:].rearrange("p (c i) t -> p c t i", i=4),
                w_raw[d][:, :, m * P : (m + 1) * P].rearrange("p t (c i) -> p c t i", i=4),
            )
            return grouped

        def quantize(grouped, codes, scales):
            nc.vector.quantize_mx(out=codes.bitcast(FP8X4), scales=scales, in_=grouped[:].rearrange("p m t -> p (m t)"))

        codes1 = keep.tile([P, N], U32, name="codes1", align_bytes=64)
        scales1 = keep.tile([P, N], U8, name="scales1", align_bytes=64)
        codes0 = keep.tile([P, N], U32, name="codes0", align_bytes=64)
        scales0 = keep.tile([P, N], U8, name="scales0", align_bytes=64)
        grouped1a = round_weights(1, 0, "grouped1a")
        grouped1b = round_weights(1, 1, "shared")
        grouped0a = round_weights(0, 0, "grouped0a")
        grouped0b = round_weights(0, 1, "grouped0b")
        quantize(grouped1a, codes1[:, :P], scales1[:, :P])
        quantize(grouped1b, codes1[:, P:], scales1[:, P:])

        late_words = keep.tile([P, LATE], U32, name="late_words", tag="shared", align_bytes=64)
        nc.vector.tensor_copy(late_words[:], table_words[:].bitcast(U32).indirect(offsets[:, : LATE // 16]))
        quantize(grouped0a, codes0[:, :P], scales0[:, :P])
        quantize(grouped0b, codes0[:, P:], scales0[:, P:])

        def words_of(first, count):
            if first < LATE:
                return late_words[:, first : first + count]
            return early_words[:, first - LATE : first - LATE + count]

        def product(acc, codes, scales, m, first, count):
            cols = slice(m * P, (m + 1) * P)
            nc.tensor.matmul_mx(
                out=acc,
                lhsT=codes[:, cols].bitcast(FP8X4),
                lhsT_scale=scales[:, cols],
                rhs=words_of(first, count).bitcast(FP8X4),
                rhs_scale=picked_scales[:, first : first + count],
                start=True,
                stop=True,
            )

        wide0 = psum.tile([P, BANK], F32, name="wide0", tag="reused")
        narrow = psum.tile([P, BANK], F32, name="narrow")
        wide1 = psum.tile([P, BANK], F32, name="wide1")
        gate_pieces = [
            (0, 0, BANK, wide0[:]),
            (0, BANK, HALF, narrow[:, :HALF]),
            (1, BANK, HALF, narrow[:, HALF:]),
            (1, 0, BANK, wide1[:]),
        ]
        for m, v0, count, y1 in gate_pieces:
            product(y1, codes1, scales1, m, V + v0, count)
        gates = {}
        for m, v0, count, y1 in gate_pieces:
            gate = keep.tile([P, count], F32, name="gate%d_%d" % (m, v0))
            nc.scalar.activation(gate[:], y1, SIGMOID, bias=bias[:, m : m + 1])
            for c in range(0, count, HALF):
                gates[m, v0 + c] = gate[:, c : c + HALF]
        for i, (m, v0) in enumerate(gates):
            tag = "reused" if i == len(gates) - 1 else "y0_%d" % i
            y0 = psum.tile([P, BANK], F32, name="y0_%d" % i, tag=tag)
            product(y0[:, :HALF], codes0, scales0, m, v0, HALF)
            result = keep.tile([P, HALF], F32, name="result%d" % i)
            nc.vector.tensor_tensor(result[:], y0[:, :HALF], gates[m, v0], MULT)
            nc.sync.dma_start(out[m * P : (m + 1) * P, v0 : v0 + HALF], result[:])
